import numpy as np
import ml_dtypes


def mxq(x, axis, fmt="e4m3"):
    dtype, down = {"e4m3": (ml_dtypes.float8_e4m3fn, 7), "e5m2": (ml_dtypes.float8_e5m2, 14)}[fmt]
    v = np.moveaxis(np.asarray(x, np.float32).astype(ml_dtypes.bfloat16).astype(np.float64), axis, -1)
    blocks = v.reshape(v.shape[:-1] + (-1, 32))
    amax = np.abs(blocks).max(-1, keepdims=True)
    byte = np.maximum(np.where(amax > 0, np.frexp(amax)[1] - 1 + 127, 0) - down, 1)
    scale = np.exp2(byte - 127.0)
    codes = (blocks / scale).astype(np.float32).astype(dtype).astype(np.float64)
    return np.moveaxis((codes * scale).reshape(v.shape), -1, axis)


WIDE = False


def mx_kscale(k):
    if not WIDE:
        return np.ones(k)
    levels = np.array([10, -10, 5, -5, 0])
    if k % 512:
        return np.exp2(np.random.permutation(np.resize(levels, k // 32))).repeat(32)
    a = np.empty((k // 512, 16))
    for p in range(k // 512):
        a[p, :8] = np.random.permutation(np.resize(levels, 8))
        for g in range(8):
            far = levels[np.abs(levels - a[p, g]) >= 10]
            a[p, g + 8] = far[np.random.randint(len(far))]
    return np.exp2(a.ravel()).repeat(32)


BF16 = ml_dtypes.bfloat16


def bf(x):
    return np.asarray(x, np.float32).astype(BF16)


def f64(x):
    return np.asarray(x).astype(np.float64)

E4M3FN = np.array([(-1.0 if i & 128 else 1.0) * ((1.0 + (i & 7) / 8.0) * 2.0 ** (((i >> 3) & 15) - 7) if i & 120 else (i & 7) * 2.0 ** -9) for i in range(256)])


def e4m3fn_bytes(y):
    return np.clip(np.asarray(y, np.float64), -448.0, 448.0).astype(np.float32).astype(ml_dtypes.float8_e4m3fn).view(np.uint8)


def e4m3fn_values(b):
    return E4M3FN[b]


K, T, M, B = 1536, 4096, 512, 1024


def setup_inputs():
    s, t = mx_kscale(K), mx_kscale(M)
    x = np.random.standard_normal((K, T)) * s[:, None]
    e = np.random.standard_normal((M, B)) / np.sqrt(M) / t[:, None]
    x_scale = (np.abs(x).max(axis=1, keepdims=True) / 448).astype(np.float32)
    e_scale = (np.abs(e).max(axis=1, keepdims=True) / 448).astype(np.float32)
    return {"X_bytes": e4m3fn_bytes(x / f64(x_scale)),
            "X_scale": x_scale,
            "P": bf(np.random.standard_normal((K, M)) / np.sqrt(K) / s[:, None] * t),
            "b": bf(0.3 * np.random.standard_normal(M) * t),
            "E_bytes": e4m3fn_bytes(e / f64(e_scale)),
            "E_scale": e_scale,
            "g": bf(1 + 0.1 * np.random.standard_normal(T))}


def reference(X_bytes, X_scale, P, b, E_bytes, E_scale, g):
    X = e4m3fn_values(X_bytes) * f64(X_scale)
    E = e4m3fn_values(E_bytes) * f64(E_scale)
    z = mxq(X, 0, "e4m3").T @ mxq(f64(P), 0, "e4m3")
    A = np.maximum(z + f64(b), 0.0)
    Y = mxq(E, 0, "e4m3").T @ mxq(A, 1, "e4m3").T
    return Y * f64(g)

@@ -1,0 +1,348 @@
+from contextlib import ExitStack
+
+import concourse.mybir as mybir
+from concourse.masks import make_identity
+
+K, T, M, B = 1536, 4096, 512, 1024
+FLOPS = 2 * T * M * (K + B)
+
+F32 = mybir.dt.float32
+BF16 = mybir.dt.bfloat16
+U32 = mybir.dt.uint32
+U8 = mybir.dt.uint8
+FP8 = mybir.dt.float8_e4m3fn
+FP8X4 = mybir.dt.float8_e4m3fn_x4
+ACT = mybir.ActivationFunctionType
+MULT = mybir.AluOpType.mult
+
+G = 3
+WIDTHS = [256] + [512] * 7 + [256]
+NC = len(WIDTHS)
+STARTS = [sum(WIDTHS[:i]) for i in range(NC)]
+LOADS = [256, 512, 1024, 1024, 1280]
+
+NV0 = 2
+NV = {1: 4, 2: 2}
+EV = (0,)
+XI = 1
+INT_P = {0: (0, 1, 2), 8: ()}
+PE_G = (0, 1)
+YB, ZB, TB = 3, 3, 2
+SPREAD = (0, 0, 0, 1, 2, 3, 5, 7, 9)
+
+
+def widen_v(c, gi, t):
+    if c == 0:
+        return gi == 0
+    return 4 * (2 - gi) + t < NV.get(c, NV0)
+
+
+def pe_g(c):
+    return INT_P.get(c, PE_G)
+
+
+def interleave(copy, dst, src):
+    copy(
+        out=dst.rearrange("p (c i) t -> p c t i", i=4),
+        in_=src.rearrange("p t (c i) -> p c t i", i=4),
+    )
+
+
+def tile_clipped_cube_unmixing_d5_kernel(tc, X_bytes, X_scale, P, b, E_bytes, E_scale, g, out):
+    nc = tc.nc
+    with ExitStack() as ctx:
+        keep = ctx.enter_context(tc.tile_pool(name="keep", bufs=1))
+        work = ctx.enter_context(tc.tile_pool(name="work", bufs=2))
+        psum = ctx.enter_context(tc.psum_pool(name="psum", bufs=1))
+        ctx.enter_context(tc.manual_schedule())
+
+        ident = keep.tile([128, 128], BF16, name="ident")
+        make_identity(nc, ident[:])
+
+        xv = X_bytes.rearrange("(g p t) n -> g p t n", p=128, t=4)
+        pv = P.rearrange("(g p t) m -> g p t m", p=128, t=4)
+        xs = keep.tile([128, G, 4], F32, name="xs")
+        nc.sync.dma_start(out=xs[:], in_=X_scale.rearrange("(g p t) o -> p g (t o)", p=128, t=4))
+
+        xbytes = {}
+        load_of = {}
+        at = 0
+        load_cols = []
+        for w in LOADS:
+            load_cols.append((at, w))
+            at += w
+
+        def load_x(l):
+            c0, w = load_cols[l]
+            for gi in range(G):
+                tl = keep.tile([128, 4, w], U8, name="xb%d_%d" % (l, gi))
+                nc.sync.dma_start(out=tl[:], in_=xv[gi][:, :, c0 : c0 + w])
+                xbytes[(l, gi)] = tl
+            for c in range(NC):
+                if c0 <= STARTS[c] and STARTS[c] + WIDTHS[c] <= c0 + w:
+                    load_of[c] = (l, STARTS[c] - c0)
+
+        praw = []
+
+        def load_p(gi):
+            tl = keep.tile([128, 4, M], BF16, name="praw%d" % gi)
+            nc.sync.dma_start(out=tl[:], in_=pv[gi])
+            praw.append(tl)
+
+        load_x(0)
+        for gi in range(G):
+            load_p(gi)
+        load_x(1)
+        bt = keep.tile([128, 4], BF16, name="bt")
+        nc.sync.dma_start(out=bt[:], in_=b.rearrange("(p t) -> p t", t=4))
+        es = keep.tile([128, 4], F32, name="es")
+        nc.sync.dma_start(out=es[:], in_=E_scale.rearrange("(p t) o -> p (t o)", t=4))
+        eb = keep.tile([128, 4, B], U8, name="eb")
+        nc.sync.dma_start(out=eb[:], in_=E_bytes.rearrange("(p t) n -> p t n", t=4))
+        load_x(2)
+        gt = keep.tile([128, T], BF16, name="gt")
+        nc.sync.dma_start(out=gt[:, 0:1024], in_=g[0:1024].partition_broadcast(128))
+        load_x(3)
+        nc.sync.dma_start(out=gt[:, 1024:T], in_=g[1024:T].partition_broadcast(128))
+        load_x(4)
+
+        pcodes = keep.tile([128, G, M], U32, name="pcodes", align_bytes=64)
+        pscales = keep.tile([128, G, M], U8, name="pscales", align_bytes=64)
+        ecodes = keep.tile([128, B], U32, name="ecodes", align_bytes=64)
+        escales = keep.tile([128, B], U8, name="escales", align_bytes=64)
+
+        wide, inter, xcodes, xscales = {}, {}, {}, {}
+
+        def widen(c, gi, t):
+            if (c, gi) not in wide:
+                wide[(c, gi)] = work.tile([128, 4, 512], BF16, name="wide", bufs=9, align_bytes=64)
+            l, off = load_of[c]
+            n = WIDTHS[c]
+            src = xbytes[(l, gi)][:, t, off : off + n].bitcast(FP8)
+            dst = wide[(c, gi)][:, t, 0:n]
+            if widen_v(c, gi, t):
+                nc.vector.tensor_scalar(out=dst, in0=src, scalar1=xs[:, gi, t : t + 1], scalar2=None, op0=MULT)
+            else:
+                nc.scalar.activation(out=dst, in_=src, func=ACT.Copy, scale=xs[:, gi, t : t + 1])
+
+        def new_inter(key):
+            if key not in inter:
+                inter[key] = work.tile([128, 512, 4], BF16, name="inter", bufs=8, align_bytes=64)
+            return inter[key]
+
+        def xint(c, gi):
+            n = WIDTHS[c]
+            interleave(nc.vector.tensor_copy, new_inter((c, gi))[:, 0:n, :], wide[(c, gi)][:, :, 0:n])
+
+        turned = {}
+
+        def pe_int(c, gi, h):
+            bank = psum.tile([128, 256, 4], BF16, name="turn", bufs=TB)
+            turned[(c, gi, h)] = bank
+            for k in range(2):
+                col = 256 * h + 128 * k
+                nc.tensor.matmul(
+                    bank[:, 128 * k : 128 * k + 128, :].rearrange("p n t -> p (n t)"),
+                    lhsT=ident[:],
+                    rhs=wide[(c, gi)][:, :, col : col + 128].rearrange("p t n -> p n t"),
+                    start=True,
+                    stop=True,
+                )
+
+        def evac(c, gi, h):
+            nc.scalar.copy(out=new_inter((c, gi))[:, 256 * h : 256 * h + 256, :], in_=turned[(c, gi, h)][:])
+
+        def quant(codes, scales, tl, n):
+            nc.vector.quantize_mx(
+                out=codes.bitcast(FP8X4), scales=scales, in_=tl[:, 0:n, :].rearrange("p n t -> p (n t)")
+            )
+
+        def xq(c, gi):
+            n = WIDTHS[c]
+            xcodes[(c, gi)] = work.tile([128, 512], U32, name="xcodes", bufs=6, align_bytes=64)
+            xscales[(c, gi)] = work.tile([128, 512], U8, name="xscales", bufs=6, align_bytes=64)
+            quant(xcodes[(c, gi)][:, 0:n], xscales[(c, gi)][:, 0:n], inter[(c, gi)], n)
+
+        def pint(gi):
+            nc.vector.tensor_copy(
+                out=new_inter(("p", gi))[:].rearrange("p (j q) t -> p j q t", j=4),
+                in_=praw[gi][:].rearrange("p t (q j) -> p j q t", j=4),
+            )
+
+        def pq(gi):
+            quant(pcodes[:, gi, :], pscales[:, gi, :], inter[("p", gi)], M)
+
+        def ewiden(h):
+            wide[("e", h)] = work.tile([128, 4, 512], BF16, name="wide", bufs=9, align_bytes=64)
+            for t in range(4):
+                dst = wide[("e", h)][:, t, :]
+                src = eb[:, t, 512 * h : 512 * h + 512].bitcast(FP8)
+                if h in EV:
+                    nc.vector.tensor_scalar(out=dst, in0=src, scalar1=es[:, t : t + 1], scalar2=None, op0=MULT)
+                else:
+                    nc.scalar.activation(out=dst, in_=src, func=ACT.Copy, scale=es[:, t : t + 1])
+
+        def eint(h):
+            interleave(nc.vector.tensor_copy, new_inter(("e", h))[:], wide[("e", h)][:])
+
+        def eq(h):
+            cols = slice(512 * h, 512 * h + 512)
+            quant(ecodes[:, cols], escales[:, cols], inter[("e", h)], 512)
+
+        zbank, planes, acodes, ascales, ybank = {}, {}, {}, {}, {}
+
+        def st1(c, js=range(4)):
+            n = WIDTHS[c]
+            for j in js:
+                zbank[(c, j)] = psum.tile([128, 512], F32, name="z", bufs=ZB)
+                cols = slice(128 * j, 128 * j + 128)
+                for gi in range(G):
+                    nc.tensor.matmul_mx(
+                        out=zbank[(c, j)][:, 0:n],
+                        lhsT=pcodes[:, gi, cols].bitcast(FP8X4),
+                        lhsT_scale=pscales[:, gi, cols],
+                        rhs=xcodes[(c, gi)][:, 0:n].bitcast(FP8X4),
+                        rhs_scale=xscales[(c, gi)][:, 0:n],
+                        start=(gi == 0),
+                        stop=(gi == G - 1),
+                    )
+
+        def relu(c, j):
+            n = WIDTHS[c]
+            if j == 0:
+                planes[c] = work.tile([128, 4, 512], BF16, name="planes", bufs=2, align_bytes=64)
+            nc.scalar.activation(
+                out=planes[c][:, j, 0:n], in_=zbank[(c, j)][:, 0:n], func=ACT.Relu, bias=bt[:, j : j + 1]
+            )
+
+        def aint(c):
+            n = WIDTHS[c]
+            interleave(nc.vector.tensor_copy, new_inter(("a", c))[:, 0:n, :], planes[c][:, :, 0:n])
+
+        def aq(c):
+            n = WIDTHS[c]
+            acodes[c] = work.tile([128, 512], U32, name="acodes", bufs=2, align_bytes=64)
+            ascales[c] = work.tile([128, 512], U8, name="ascales", bufs=2, align_bytes=64)
+            quant(acodes[c][:, 0:n], ascales[c][:, 0:n], inter[("a", c)], n)
+
+        def st2(c, m):
+            n = WIDTHS[c]
+            ybank[(c, m)] = psum.tile([128, 512], F32, name="y", bufs=YB)
+            cols = slice(128 * m, 128 * m + 128)
+            nc.tensor.matmul_mx(
+                out=ybank[(c, m)][:, 0:n],
+                lhsT=ecodes[:, cols].bitcast(FP8X4),
+                lhsT_scale=escales[:, cols],
+                rhs=acodes[c][:, 0:n].bitcast(FP8X4),
+                rhs_scale=ascales[c][:, 0:n],
+                start=True,
+                stop=True,
+            )
+
+        def y(c, m):
+            n = WIDTHS[c]
+            cols = slice(STARTS[c], STARTS[c] + n)
+            yt = work.tile([128, 512], F32, name="yt", bufs=10)
+            nc.vector.tensor_tensor(out=yt[:, 0:n], in0=ybank[(c, m)][:, 0:n], in1=gt[:, cols], op=MULT)
+            nc.sync.dma_start(out=out[128 * m : 128 * m + 128, cols], in_=yt[:, 0:n])
+
+        for t in range(4):
+            widen(0, 0, t)
+        for gi in (1, 2):
+            for t in range(4):
+                widen(0, gi, t)
+        pint(0)
+        for gi in (1, 2, 0):
+            pe_int(0, gi, 0)
+            evac(0, gi, 0)
+        first = [(1, gi, t) for gi in range(G) for t in range(4)]
+        for w in first:
+            if not widen_v(*w):
+                widen(*w)
+        for h in range(2):
+            if h not in EV:
+                ewiden(h)
+        xq(0, 1)
+        pq(0)
+        pint(1)
+        xq(0, 2)
+        pq(1)
+        pint(2)
+        xq(0, 0)
+        pq(2)
+        st1(0)
+        for w in first:
+            if widen_v(*w):
+                widen(*w)
+        for h in EV:
+            ewiden(h)
+
+        for i in range(NC + 1):
+            prev, nxt, far = i - 1, i + 1, i + 2
+            turns = [(nxt, gi, h) for gi in pe_g(nxt) for h in range(WIDTHS[nxt] // 256)] if nxt < NC else []
+            wides = [(far, gi, t) for gi in (0, 2, 1) for t in range(4)] if far < NC else []
+            wides_v = [w for w in wides if widen_v(*w)]
+            wides_s = [w for w in wides if not widen_v(*w)]
+            if i == 0:
+                eint(0)
+                eint(1)
+                eq(0)
+                eq(1)
+                relu(0, 0)
+
+            def evac_next(k):
+                if k < len(turns):
+                    evac(*turns[k])
+                    if k + TB < len(turns):
+                        pe_int(*turns[k + TB])
+
+            def spread(k):
+                lo, hi = SPREAD[k], SPREAD[k + 1]
+                for w in wides_s[len(wides_s) * lo // SPREAD[-1] : len(wides_s) * hi // SPREAD[-1]]:
+                    widen(*w)
+
+            for s in range(8):
+                if s == 0:
+                    if 0 < i < NC:
+                        st1(i, [3])
+                    for x in turns[0:TB]:
+                        pe_int(*x)
+                    if i < NC:
+                        relu(i, 1)
+                        relu(i, 2)
+                if s == 1:
+                    if i < NC:
+                        relu(i, 3)
+                    evac_next(0)
+                if s in (2, 3, 4):
+                    evac_next(s - 1)
+                spread(s)
+                if prev >= 0:
+                    y(prev, s)
+                    if s + YB < 8:
+                        st2(prev, s + YB)
+                    elif i < NC:
+                        st2(i, s + YB - 8)
+                elif s + YB >= 8:
+                    st2(i, s + YB - 8)
+                if s == XI and nxt < NC:
+                    for gi in range(G):
+                        if gi not in pe_g(nxt):
+                            xint(nxt, gi)
+                if s == XI + 1 and nxt < NC:
+                    xq(nxt, 2)
+                if s == 2 and nxt < NC:
+                    xq(nxt, 0)
+                if s == 3 and i < NC:
+                    aint(i)
+                if s == 4 and i < NC:
+                    aq(i)
+                if s == 5 and nxt < NC:
+                    xq(nxt, 1)
+                if s >= 5 and nxt < NC:
+                    st1(nxt, [s - 5])
+                if s == 7 and nxt < NC:
+                    relu(nxt, 0)
+                if s >= 6:
+                    for w in wides_v[s - 6 :: 2]:
+                        widen(*w)

@@ -21,14 +21,15 @@ NC = len(WIDTHS)
 STARTS = [sum(WIDTHS[:i]) for i in range(NC)]
 LOADS = [256, 512, 1024, 1024, 1280]
 
-NV0 = 2
-NV = {1: 4, 2: 2}
+NV0 = 1
+NV = {1: 2, 2: 1}
 EV = (0,)
 XI = 1
-INT_P = {0: (0, 1, 2), 8: ()}
-PE_G = (0, 1)
-YB, ZB, TB = 3, 3, 2
-SPREAD = (0, 0, 0, 1, 2, 3, 5, 7, 9)
+INT_P = {}
+PE_G = ()
+INT_S = {(c, 1) for c in (0, 2, 3, 4, 5, 6, 7, 8)}
+YB, ZB, TB = 4, 4, 2
+SPREAD = (0, 1, 2, 3, 4, 5, 6, 7, 8)
 
 
 def widen_v(c, gi, t):
@@ -134,10 +135,14 @@ def tile_clipped_cube_unmixing_d5_kernel(tc, X_bytes, X_scale, P, b, E_bytes, E_
             n = WIDTHS[c]
             interleave(nc.vector.tensor_copy, new_inter((c, gi))[:, 0:n, :], wide[(c, gi)][:, :, 0:n])
 
+        def sint(c, gi):
+            n = WIDTHS[c]
+            interleave(nc.scalar.copy, new_inter((c, gi))[:, 0:n, :], wide[(c, gi)][:, :, 0:n])
+
         turned = {}
 
         def pe_int(c, gi, h):
-            bank = psum.tile([128, 256, 4], BF16, name="turn", bufs=TB)
+            bank = psum.tile([128, 256, 4], BF16, name="turn", bufs=2)
             turned[(c, gi, h)] = bank
             for k in range(2):
                 col = 256 * h + 128 * k
@@ -252,13 +257,18 @@ def tile_clipped_cube_unmixing_d5_kernel(tc, X_bytes, X_scale, P, b, E_bytes, E_
             for t in range(4):
                 widen(0, gi, t)
         pint(0)
-        for gi in (1, 2, 0):
-            pe_int(0, gi, 0)
-            evac(0, gi, 0)
+        if (0, 1) in INT_S:
+            sint(0, 1)
+        else:
+            xint(0, 1)
+        xint(0, 0)
+        xint(0, 2)
         first = [(1, gi, t) for gi in range(G) for t in range(4)]
         for w in first:
             if not widen_v(*w):
                 widen(*w)
+        if (1, 1) in INT_S:
+            sint(1, 1)
         for h in range(2):
             if h not in EV:
                 ewiden(h)
@@ -283,6 +293,7 @@ def tile_clipped_cube_unmixing_d5_kernel(tc, X_bytes, X_scale, P, b, E_bytes, E_
             wides = [(far, gi, t) for gi in (0, 2, 1) for t in range(4)] if far < NC else []
             wides_v = [w for w in wides if widen_v(*w)]
             wides_s = [w for w in wides if not widen_v(*w)]
+            wides_s += [(far, gi) for gi in range(G) if (far, gi) in INT_S]
             if i == 0:
                 eint(0)
                 eint(1)
@@ -299,7 +310,10 @@ def tile_clipped_cube_unmixing_d5_kernel(tc, X_bytes, X_scale, P, b, E_bytes, E_
             def spread(k):
                 lo, hi = SPREAD[k], SPREAD[k + 1]
                 for w in wides_s[len(wides_s) * lo // SPREAD[-1] : len(wides_s) * hi // SPREAD[-1]]:
-                    widen(*w)
+                    if len(w) == 2:
+                        sint(*w)
+                    else:
+                        widen(*w)
 
             for s in range(8):
                 if s == 0:
@@ -319,24 +333,23 @@ def tile_clipped_cube_unmixing_d5_kernel(tc, X_bytes, X_scale, P, b, E_bytes, E_
                 spread(s)
                 if prev >= 0:
                     y(prev, s)
-                    if s + YB < 8:
-                        st2(prev, s + YB)
-                    elif i < NC:
-                        st2(i, s + YB - 8)
-                elif s + YB >= 8:
-                    st2(i, s + YB - 8)
-                if s == XI and nxt < NC:
-                    for gi in range(G):
-                        if gi not in pe_g(nxt):
-                            xint(nxt, gi)
-                if s == XI + 1 and nxt < NC:
-                    xq(nxt, 2)
-                if s == 2 and nxt < NC:
-                    xq(nxt, 0)
+                if s in (0, 1, 2) and nxt < NC:
+                    gi = (0, 2, 1)[s]
+                    if (nxt, gi) not in INT_S:
+                        xint(nxt, gi)
+                    if s == 1:
+                        xq(nxt, 0)
+                    if s == 2:
+                        xq(nxt, 2)
                 if s == 3 and i < NC:
                     aint(i)
                 if s == 4 and i < NC:
                     aq(i)
+                if s + YB < 8:
+                    if prev >= 0:
+                        st2(prev, s + YB)
+                elif i < NC:
+                    st2(i, s + YB - 8)
                 if s == 5 and nxt < NC:
                     xq(nxt, 1)
                 if s >= 5 and nxt < NC:

@@ -1,7 +1,6 @@
 from contextlib import ExitStack
 
 import concourse.mybir as mybir
-from concourse.masks import make_identity
 
 K, T, M, B = 1536, 4096, 512, 1024
 FLOPS = 2 * T * M * (K + B)
@@ -21,25 +20,20 @@ NC = len(WIDTHS)
 STARTS = [sum(WIDTHS[:i]) for i in range(NC)]
 LOADS = [256, 512, 1024, 1024, 1280]
 
-NV0 = 1
-NV = {1: 2, 2: 1}
-EV = (0,)
-XI = 1
-INT_P = {}
-PE_G = ()
-INT_S = {(c, 1) for c in (0, 2, 3, 4, 5, 6, 7, 8)}
-YB, ZB, TB = 4, 4, 2
-SPREAD = (0, 1, 2, 3, 4, 5, 6, 7, 8)
+NV = [12,0,4,3,1,3,1,0,0]
+HOW = ["SSV","SVS","VVV","VSV","VSV","SVV","VSV","VSV","VSS"]
+EV = (0, 1)
+EHOW = "VV"
+AS = (0, 8)
+YB, ZB = 4, 4
+SPREAD = (0, 2, 2, 4, 4, 9, 10, 11, 12)
+GORD = (0, 1, 2)
 
 
 def widen_v(c, gi, t):
     if c == 0:
-        return gi == 0
-    return 4 * (2 - gi) + t < NV.get(c, NV0)
-
-
-def pe_g(c):
-    return INT_P.get(c, PE_G)
+        return 4 * gi + t < NV[0]
+    return 4 * (2 - gi) + t < NV[c]
 
 
 def interleave(copy, dst, src):
@@ -57,13 +51,10 @@ def tile_clipped_cube_unmixing_d5_kernel(tc, X_bytes, X_scale, P, b, E_bytes, E_
         psum = ctx.enter_context(tc.psum_pool(name="psum", bufs=1))
         ctx.enter_context(tc.manual_schedule())
 
-        ident = keep.tile([128, 128], BF16, name="ident")
-        make_identity(nc, ident[:])
-
         xv = X_bytes.rearrange("(g p t) n -> g p t n", p=128, t=4)
         pv = P.rearrange("(g p t) m -> g p t m", p=128, t=4)
         xs = keep.tile([128, G, 4], F32, name="xs")
-        nc.sync.dma_start(out=xs[:], in_=X_scale.rearrange("(g p t) o -> p g (t o)", p=128, t=4))
+        nc.scalar.dma_start(out=xs[:], in_=X_scale.rearrange("(g p t) o -> p g (t o)", p=128, t=4))
 
         xbytes = {}
         load_of = {}
@@ -73,9 +64,9 @@ def tile_clipped_cube_unmixing_d5_kernel(tc, X_bytes, X_scale, P, b, E_bytes, E_
             load_cols.append((at, w))
             at += w
 
-        def load_x(l):
+        def load_x(l, gs=range(G)):
             c0, w = load_cols[l]
-            for gi in range(G):
+            for gi in gs:
                 tl = keep.tile([128, 4, w], U8, name="xb%d_%d" % (l, gi))
                 nc.sync.dma_start(out=tl[:], in_=xv[gi][:, :, c0 : c0 + w])
                 xbytes[(l, gi)] = tl
@@ -93,16 +84,16 @@ def tile_clipped_cube_unmixing_d5_kernel(tc, X_bytes, X_scale, P, b, E_bytes, E_
         load_x(0)
         for gi in range(G):
             load_p(gi)
-        load_x(1)
+            load_x(1, [gi])
         bt = keep.tile([128, 4], BF16, name="bt")
-        nc.sync.dma_start(out=bt[:], in_=b.rearrange("(p t) -> p t", t=4))
+        nc.scalar.dma_start(out=bt[:], in_=b.rearrange("(p t) -> p t", t=4))
         es = keep.tile([128, 4], F32, name="es")
-        nc.sync.dma_start(out=es[:], in_=E_scale.rearrange("(p t) o -> p (t o)", t=4))
+        nc.scalar.dma_start(out=es[:], in_=E_scale.rearrange("(p t) o -> p (t o)", t=4))
         eb = keep.tile([128, 4, B], U8, name="eb")
         nc.sync.dma_start(out=eb[:], in_=E_bytes.rearrange("(p t) n -> p t n", t=4))
-        load_x(2)
         gt = keep.tile([128, T], BF16, name="gt")
         nc.sync.dma_start(out=gt[:, 0:1024], in_=g[0:1024].partition_broadcast(128))
+        load_x(2)
         load_x(3)
         nc.sync.dma_start(out=gt[:, 1024:T], in_=g[1024:T].partition_broadcast(128))
         load_x(4)
@@ -138,24 +129,6 @@ def tile_clipped_cube_unmixing_d5_kernel(tc, X_bytes, X_scale, P, b, E_bytes, E_
         def sint(c, gi):
             n = WIDTHS[c]
             interleave(nc.scalar.copy, new_inter((c, gi))[:, 0:n, :], wide[(c, gi)][:, :, 0:n])
-
-        turned = {}
-
-        def pe_int(c, gi, h):
-            bank = psum.tile([128, 256, 4], BF16, name="turn", bufs=2)
-            turned[(c, gi, h)] = bank
-            for k in range(2):
-                col = 256 * h + 128 * k
-                nc.tensor.matmul(
-                    bank[:, 128 * k : 128 * k + 128, :].rearrange("p n t -> p (n t)"),
-                    lhsT=ident[:],
-                    rhs=wide[(c, gi)][:, :, col : col + 128].rearrange("p t n -> p n t"),
-                    start=True,
-                    stop=True,
-                )
-
-        def evac(c, gi, h):
-            nc.scalar.copy(out=new_inter((c, gi))[:, 256 * h : 256 * h + 256, :], in_=turned[(c, gi, h)][:])
 
         def quant(codes, scales, tl, n):
             nc.vector.quantize_mx(
@@ -194,6 +167,8 @@ def tile_clipped_cube_unmixing_d5_kernel(tc, X_bytes, X_scale, P, b, E_bytes, E_
             cols = slice(512 * h, 512 * h + 512)
             quant(ecodes[:, cols], escales[:, cols], inter[("e", h)], 512)
 
+        yv = out.rearrange("(m p) n -> p m n", p=128)
+        ytile = {}
         zbank, planes, acodes, ascales, ybank = {}, {}, {}, {}, {}
 
         def st1(c, js=range(4)):
@@ -222,7 +197,8 @@ def tile_clipped_cube_unmixing_d5_kernel(tc, X_bytes, X_scale, P, b, E_bytes, E_
 
         def aint(c):
             n = WIDTHS[c]
-            interleave(nc.vector.tensor_copy, new_inter(("a", c))[:, 0:n, :], planes[c][:, :, 0:n])
+            copy = nc.scalar.copy if c in AS else nc.vector.tensor_copy
+            interleave(copy, new_inter(("a", c))[:, 0:n, :], planes[c][:, :, 0:n])
 
         def aq(c):
             n = WIDTHS[c]
@@ -247,115 +223,130 @@ def tile_clipped_cube_unmixing_d5_kernel(tc, X_bytes, X_scale, P, b, E_bytes, E_
         def y(c, m):
             n = WIDTHS[c]
             cols = slice(STARTS[c], STARTS[c] + n)
-            yt = work.tile([128, 512], F32, name="yt", bufs=10)
-            nc.vector.tensor_tensor(out=yt[:, 0:n], in0=ybank[(c, m)][:, 0:n], in1=gt[:, cols], op=MULT)
-            nc.sync.dma_start(out=out[128 * m : 128 * m + 128, cols], in_=yt[:, 0:n])
+            if m % 2 == 0:
+                ytile[c] = work.tile([128, 2, 512], F32, name="yt", bufs=5)
+            dst = ytile[c][:, m % 2, 0:n]
+            nc.vector.tensor_tensor(out=dst, in0=ybank[(c, m)][:, 0:n], in1=gt[:, cols], op=MULT)
+            if c == NC - 1 and m >= 4:
+                nc.sync.dma_start(out=yv[:, m, cols], in_=dst)
+            elif m % 2 == 1:
+                nc.sync.dma_start(out=yv[:, m - 1 : m + 1, cols], in_=ytile[c][:, :, 0:n])
 
-        for t in range(4):
-            widen(0, 0, t)
-        for gi in (1, 2):
-            for t in range(4):
-                widen(0, gi, t)
-        pint(0)
-        if (0, 1) in INT_S:
-            sint(0, 1)
-        else:
-            xint(0, 1)
-        xint(0, 0)
-        xint(0, 2)
-        first = [(1, gi, t) for gi in range(G) for t in range(4)]
-        for w in first:
-            if not widen_v(*w):
-                widen(*w)
-        if (1, 1) in INT_S:
-            sint(1, 1)
+        def s_list(c):
+            ops = []
+            for gi in GORD:
+                ops += [("w", c, gi, t) for t in range(4) if not widen_v(c, gi, t)]
+                if HOW[c][gi] == "S":
+                    ops.append(("i", c, gi))
+            return [o for o in ops if o[0] == "w"] + [o for o in ops if o[0] == "i"]
+
+        def v_list(c):
+            return [(c, gi, t) for gi in GORD for t in range(4) if widen_v(c, gi, t)]
+
+        def s_run(op):
+            if op[0] == "w":
+                widen(*op[1:])
+            else:
+                sint(*op[1:])
+
+        for w in v_list(0):
+            widen(*w)
+        for o in s_list(0):
+            s_run(o)
+        first_v = v_list(1)
+        late = []
+        for o in s_list(1):
+            if o[0] == "w":
+                s_run(o)
+            else:
+                late.append(o)
         for h in range(2):
             if h not in EV:
                 ewiden(h)
-        xq(0, 1)
+        if HOW[0][0] == "V":
+            xint(0, 0)
+        pint(0)
+        if HOW[0][1] == "V":
+            xint(0, 1)
+        xq(0, 0)
         pq(0)
         pint(1)
-        xq(0, 2)
+        if HOW[0][2] == "V":
+            xint(0, 2)
+        xq(0, 1)
         pq(1)
+        for w in first_v[:4]:
+            widen(*w)
         pint(2)
-        xq(0, 0)
+        xq(0, 2)
         pq(2)
         st1(0)
-        for w in first:
-            if widen_v(*w):
-                widen(*w)
+        for w in first_v[4:]:
+            widen(*w)
         for h in EV:
             ewiden(h)
+        for o in late:
+            s_run(o)
+        for h in range(2):
+            if EHOW[h] == "S":
+                interleave(nc.scalar.copy, new_inter(("e", h))[:], wide[("e", h)][:])
 
         for i in range(NC + 1):
             prev, nxt, far = i - 1, i + 1, i + 2
-            turns = [(nxt, gi, h) for gi in pe_g(nxt) for h in range(WIDTHS[nxt] // 256)] if nxt < NC else []
-            wides = [(far, gi, t) for gi in (0, 2, 1) for t in range(4)] if far < NC else []
-            wides_v = [w for w in wides if widen_v(*w)]
-            wides_s = [w for w in wides if not widen_v(*w)]
-            wides_s += [(far, gi) for gi in range(G) if (far, gi) in INT_S]
+            wides_v = v_list(far) if far < NC else []
+            wides_s = s_list(far) if far < NC else []
             if i == 0:
-                eint(0)
-                eint(1)
-                eq(0)
-                eq(1)
-                relu(0, 0)
-
-            def evac_next(k):
-                if k < len(turns):
-                    evac(*turns[k])
-                    if k + TB < len(turns):
-                        pe_int(*turns[k + TB])
+                for h in range(2):
+                    if EHOW[h] == "V":
+                        eint(h)
+                for h in range(2):
+                    eq(h)
 
             def spread(k):
                 lo, hi = SPREAD[k], SPREAD[k + 1]
-                for w in wides_s[len(wides_s) * lo // SPREAD[-1] : len(wides_s) * hi // SPREAD[-1]]:
-                    if len(w) == 2:
-                        sint(*w)
-                    else:
-                        widen(*w)
+                for o in wides_s[len(wides_s) * lo // SPREAD[-1] : len(wides_s) * hi // SPREAD[-1]]:
+                    s_run(o)
 
             for s in range(8):
                 if s == 0:
                     if 0 < i < NC:
                         st1(i, [3])
-                    for x in turns[0:TB]:
-                        pe_int(*x)
                     if i < NC:
-                        relu(i, 1)
-                        relu(i, 2)
-                if s == 1:
-                    if i < NC:
-                        relu(i, 3)
-                    evac_next(0)
-                if s in (2, 3, 4):
-                    evac_next(s - 1)
+                        for j in range(0 if i < 2 else 1, 4):
+                            relu(i, j)
+                        if i in AS:
+                            aint(i)
                 spread(s)
                 if prev >= 0:
                     y(prev, s)
-                if s in (0, 1, 2) and nxt < NC:
-                    gi = (0, 2, 1)[s]
-                    if (nxt, gi) not in INT_S:
-                        xint(nxt, gi)
+                if nxt < NC:
+                    if s == 0 and HOW[nxt][0] == "V":
+                        xint(nxt, 0)
                     if s == 1:
+                        if HOW[nxt][2] == "V":
+                            xint(nxt, 2)
                         xq(nxt, 0)
                     if s == 2:
+                        if HOW[nxt][1] == "V":
+                            xint(nxt, 1)
                         xq(nxt, 2)
-                if s == 3 and i < NC:
-                    aint(i)
-                if s == 4 and i < NC:
-                    aq(i)
+                if i < NC:
+                    if s == 3 and i not in AS:
+                        aint(i)
+                    if s == 4:
+                        aq(i)
                 if s + YB < 8:
                     if prev >= 0:
                         st2(prev, s + YB)
                 elif i < NC:
                     st2(i, s + YB - 8)
-                if s == 5 and nxt < NC:
-                    xq(nxt, 1)
-                if s >= 5 and nxt < NC:
-                    st1(nxt, [s - 5])
-                if s == 7 and nxt < NC:
-                    relu(nxt, 0)
+                if nxt < NC:
+                    if s == 5:
+                        xq(nxt, 1)
+                    if s >= 5:
+                        st1(nxt, [s - 5])
+                    if s == 7 and i > 0:
+                        relu(nxt, 0)
                 if s >= 6:
                     for w in wides_v[s - 6 :: 2]:
                         widen(*w)

from contextlib import ExitStack

import concourse.mybir as mybir

K, T, M, B = 1536, 4096, 512, 1024
FLOPS = 2 * T * M * (K + B)

F32 = mybir.dt.float32
BF16 = mybir.dt.bfloat16
U32 = mybir.dt.uint32
U8 = mybir.dt.uint8
FP8 = mybir.dt.float8_e4m3fn
FP8X4 = mybir.dt.float8_e4m3fn_x4
ACT = mybir.ActivationFunctionType
MULT = mybir.AluOpType.mult

G = 3
WIDTHS = [256] + [512] * 7 + [256]
NC = len(WIDTHS)
STARTS = [sum(WIDTHS[:i]) for i in range(NC)]
LOADS = [256, 512, 1024, 1024, 1280]

NV = [12,0,4,3,1,3,1,0,0]
HOW = ["SSV","SVS","VVV","VSV","VSV","SVV","VSV","VSV","VSS"]
EV = (0, 1)
EHOW = "VV"
AS = (0, 8)
YB, ZB = 4, 4
SPREAD = (0, 2, 2, 4, 4, 9, 10, 11, 12)
GORD = (0, 1, 2)


def widen_v(c, gi, t):
    if c == 0:
        return 4 * gi + t < NV[0]
    return 4 * (2 - gi) + t < NV[c]


def interleave(copy, dst, src):
    copy(
        out=dst.rearrange("p (c i) t -> p c t i", i=4),
        in_=src.rearrange("p t (c i) -> p c t i", i=4),
    )


def tile_clipped_cube_unmixing_d5_kernel(tc, X_bytes, X_scale, P, b, E_bytes, E_scale, g, out):
    nc = tc.nc
    with ExitStack() as ctx:
        keep = ctx.enter_context(tc.tile_pool(name="keep", bufs=1))
        work = ctx.enter_context(tc.tile_pool(name="work", bufs=2))
        psum = ctx.enter_context(tc.psum_pool(name="psum", bufs=1))
        ctx.enter_context(tc.manual_schedule())

        xv = X_bytes.rearrange("(g p t) n -> g p t n", p=128, t=4)
        pv = P.rearrange("(g p t) m -> g p t m", p=128, t=4)
        xs = keep.tile([128, G, 4], F32, name="xs")
        nc.scalar.dma_start(out=xs[:], in_=X_scale.rearrange("(g p t) o -> p g (t o)", p=128, t=4))

        xbytes = {}
        load_of = {}
        at = 0
        load_cols = []
        for w in LOADS:
            load_cols.append((at, w))
            at += w

        def load_x(l, gs=range(G)):
            c0, w = load_cols[l]
            for gi in gs:
                tl = keep.tile([128, 4, w], U8, name="xb%d_%d" % (l, gi))
                nc.sync.dma_start(out=tl[:], in_=xv[gi][:, :, c0 : c0 + w])
                xbytes[(l, gi)] = tl
            for c in range(NC):
                if c0 <= STARTS[c] and STARTS[c] + WIDTHS[c] <= c0 + w:
                    load_of[c] = (l, STARTS[c] - c0)

        praw = []

        def load_p(gi):
            tl = keep.tile([128, 4, M], BF16, name="praw%d" % gi)
            nc.sync.dma_start(out=tl[:], in_=pv[gi])
            praw.append(tl)

        load_x(0)
        for gi in range(G):
            load_p(gi)
            load_x(1, [gi])
        bt = keep.tile([128, 4], BF16, name="bt")
        nc.scalar.dma_start(out=bt[:], in_=b.rearrange("(p t) -> p t", t=4))
        es = keep.tile([128, 4], F32, name="es")
        nc.scalar.dma_start(out=es[:], in_=E_scale.rearrange("(p t) o -> p (t o)", t=4))
        eb = keep.tile([128, 4, B], U8, name="eb")
        nc.sync.dma_start(out=eb[:], in_=E_bytes.rearrange("(p t) n -> p t n", t=4))
        gt = keep.tile([128, T], BF16, name="gt")
        nc.sync.dma_start(out=gt[:, 0:1024], in_=g[0:1024].partition_broadcast(128))
        load_x(2)
        load_x(3)
        nc.sync.dma_start(out=gt[:, 1024:T], in_=g[1024:T].partition_broadcast(128))
        load_x(4)

        pcodes = keep.tile([128, G, M], U32, name="pcodes", align_bytes=64)
        pscales = keep.tile([128, G, M], U8, name="pscales", align_bytes=64)
        ecodes = keep.tile([128, B], U32, name="ecodes", align_bytes=64)
        escales = keep.tile([128, B], U8, name="escales", align_bytes=64)

        wide, inter, xcodes, xscales = {}, {}, {}, {}

        def widen(c, gi, t):
            if (c, gi) not in wide:
                wide[(c, gi)] = work.tile([128, 4, 512], BF16, name="wide", bufs=9, align_bytes=64)
            l, off = load_of[c]
            n = WIDTHS[c]
            src = xbytes[(l, gi)][:, t, off : off + n].bitcast(FP8)
            dst = wide[(c, gi)][:, t, 0:n]
            if widen_v(c, gi, t):
                nc.vector.tensor_scalar(out=dst, in0=src, scalar1=xs[:, gi, t : t + 1], scalar2=None, op0=MULT)
            else:
                nc.scalar.activation(out=dst, in_=src, func=ACT.Copy, scale=xs[:, gi, t : t + 1])

        def new_inter(key):
            if key not in inter:
                inter[key] = work.tile([128, 512, 4], BF16, name="inter", bufs=8, align_bytes=64)
            return inter[key]

        def xint(c, gi):
            n = WIDTHS[c]
            interleave(nc.vector.tensor_copy, new_inter((c, gi))[:, 0:n, :], wide[(c, gi)][:, :, 0:n])

        def sint(c, gi):
            n = WIDTHS[c]
            interleave(nc.scalar.copy, new_inter((c, gi))[:, 0:n, :], wide[(c, gi)][:, :, 0:n])

        def quant(codes, scales, tl, n):
            nc.vector.quantize_mx(
                out=codes.bitcast(FP8X4), scales=scales, in_=tl[:, 0:n, :].rearrange("p n t -> p (n t)")
            )

        def xq(c, gi):
            n = WIDTHS[c]
            xcodes[(c, gi)] = work.tile([128, 512], U32, name="xcodes", bufs=6, align_bytes=64)
            xscales[(c, gi)] = work.tile([128, 512], U8, name="xscales", bufs=6, align_bytes=64)
            quant(xcodes[(c, gi)][:, 0:n], xscales[(c, gi)][:, 0:n], inter[(c, gi)], n)

        def pint(gi):
            nc.vector.tensor_copy(
                out=new_inter(("p", gi))[:].rearrange("p (j q) t -> p j q t", j=4),
                in_=praw[gi][:].rearrange("p t (q j) -> p j q t", j=4),
            )

        def pq(gi):
            quant(pcodes[:, gi, :], pscales[:, gi, :], inter[("p", gi)], M)

        def ewiden(h):
            wide[("e", h)] = work.tile([128, 4, 512], BF16, name="wide", bufs=9, align_bytes=64)
            for t in range(4):
                dst = wide[("e", h)][:, t, :]
                src = eb[:, t, 512 * h : 512 * h + 512].bitcast(FP8)
                if h in EV:
                    nc.vector.tensor_scalar(out=dst, in0=src, scalar1=es[:, t : t + 1], scalar2=None, op0=MULT)
                else:
                    nc.scalar.activation(out=dst, in_=src, func=ACT.Copy, scale=es[:, t : t + 1])

        def eint(h):
            interleave(nc.vector.tensor_copy, new_inter(("e", h))[:], wide[("e", h)][:])

        def eq(h):
            cols = slice(512 * h, 512 * h + 512)
            quant(ecodes[:, cols], escales[:, cols], inter[("e", h)], 512)

        yv = out.rearrange("(m p) n -> p m n", p=128)
        ytile = {}
        zbank, planes, acodes, ascales, ybank = {}, {}, {}, {}, {}

        def st1(c, js=range(4)):
            n = WIDTHS[c]
            for j in js:
                zbank[(c, j)] = psum.tile([128, 512], F32, name="z", bufs=ZB)
                cols = slice(128 * j, 128 * j + 128)
                for gi in range(G):
                    nc.tensor.matmul_mx(
                        out=zbank[(c, j)][:, 0:n],
                        lhsT=pcodes[:, gi, cols].bitcast(FP8X4),
                        lhsT_scale=pscales[:, gi, cols],
                        rhs=xcodes[(c, gi)][:, 0:n].bitcast(FP8X4),
                        rhs_scale=xscales[(c, gi)][:, 0:n],
                        start=(gi == 0),
                        stop=(gi == G - 1),
                    )

        def relu(c, j):
            n = WIDTHS[c]
            if j == 0:
                planes[c] = work.tile([128, 4, 512], BF16, name="planes", bufs=2, align_bytes=64)
            nc.scalar.activation(
                out=planes[c][:, j, 0:n], in_=zbank[(c, j)][:, 0:n], func=ACT.Relu, bias=bt[:, j : j + 1]
            )

        def aint(c):
            n = WIDTHS[c]
            copy = nc.scalar.copy if c in AS else nc.vector.tensor_copy
            interleave(copy, new_inter(("a", c))[:, 0:n, :], planes[c][:, :, 0:n])

        def aq(c):
            n = WIDTHS[c]
            acodes[c] = work.tile([128, 512], U32, name="acodes", bufs=2, align_bytes=64)
            ascales[c] = work.tile([128, 512], U8, name="ascales", bufs=2, align_bytes=64)
            quant(acodes[c][:, 0:n], ascales[c][:, 0:n], inter[("a", c)], n)

        def st2(c, m):
            n = WIDTHS[c]
            ybank[(c, m)] = psum.tile([128, 512], F32, name="y", bufs=YB)
            cols = slice(128 * m, 128 * m + 128)
            nc.tensor.matmul_mx(
                out=ybank[(c, m)][:, 0:n],
                lhsT=ecodes[:, cols].bitcast(FP8X4),
                lhsT_scale=escales[:, cols],
                rhs=acodes[c][:, 0:n].bitcast(FP8X4),
                rhs_scale=ascales[c][:, 0:n],
                start=True,
                stop=True,
            )

        def y(c, m):
            n = WIDTHS[c]
            cols = slice(STARTS[c], STARTS[c] + n)
            if m % 2 == 0:
                ytile[c] = work.tile([128, 2, 512], F32, name="yt", bufs=5)
            dst = ytile[c][:, m % 2, 0:n]
            nc.vector.tensor_tensor(out=dst, in0=ybank[(c, m)][:, 0:n], in1=gt[:, cols], op=MULT)
            if c == NC - 1 and m >= 4:
                nc.sync.dma_start(out=yv[:, m, cols], in_=dst)
            elif m % 2 == 1:
                nc.sync.dma_start(out=yv[:, m - 1 : m + 1, cols], in_=ytile[c][:, :, 0:n])

        def s_list(c):
            ops = []
            for gi in GORD:
                ops += [("w", c, gi, t) for t in range(4) if not widen_v(c, gi, t)]
                if HOW[c][gi] == "S":
                    ops.append(("i", c, gi))
            return [o for o in ops if o[0] == "w"] + [o for o in ops if o[0] == "i"]

        def v_list(c):
            return [(c, gi, t) for gi in GORD for t in range(4) if widen_v(c, gi, t)]

        def s_run(op):
            if op[0] == "w":
                widen(*op[1:])
            else:
                sint(*op[1:])

        for w in v_list(0):
            widen(*w)
        for o in s_list(0):
            s_run(o)
        first_v = v_list(1)
        late = []
        for o in s_list(1):
            if o[0] == "w":
                s_run(o)
            else:
                late.append(o)
        for h in range(2):
            if h not in EV:
                ewiden(h)
        if HOW[0][0] == "V":
            xint(0, 0)
        pint(0)
        if HOW[0][1] == "V":
            xint(0, 1)
        xq(0, 0)
        pq(0)
        pint(1)
        if HOW[0][2] == "V":
            xint(0, 2)
        xq(0, 1)
        pq(1)
        for w in first_v[:4]:
            widen(*w)
        pint(2)
        xq(0, 2)
        pq(2)
        st1(0)
        for w in first_v[4:]:
            widen(*w)
        for h in EV:
            ewiden(h)
        for o in late:
            s_run(o)
        for h in range(2):
            if EHOW[h] == "S":
                interleave(nc.scalar.copy, new_inter(("e", h))[:], wide[("e", h)][:])

        for i in range(NC + 1):
            prev, nxt, far = i - 1, i + 1, i + 2
            wides_v = v_list(far) if far < NC else []
            wides_s = s_list(far) if far < NC else []
            if i == 0:
                for h in range(2):
                    if EHOW[h] == "V":
                        eint(h)
                for h in range(2):
                    eq(h)

            def spread(k):
                lo, hi = SPREAD[k], SPREAD[k + 1]
                for o in wides_s[len(wides_s) * lo // SPREAD[-1] : len(wides_s) * hi // SPREAD[-1]]:
                    s_run(o)

            for s in range(8):
                if s == 0:
                    if 0 < i < NC:
                        st1(i, [3])
                    if i < NC:
                        for j in range(0 if i < 2 else 1, 4):
                            relu(i, j)
                        if i in AS:
                            aint(i)
                spread(s)
                if prev >= 0:
                    y(prev, s)
                if nxt < NC:
                    if s == 0 and HOW[nxt][0] == "V":
                        xint(nxt, 0)
                    if s == 1:
                        if HOW[nxt][2] == "V":
                            xint(nxt, 2)
                        xq(nxt, 0)
                    if s == 2:
                        if HOW[nxt][1] == "V":
                            xint(nxt, 1)
                        xq(nxt, 2)
                if i < NC:
                    if s == 3 and i not in AS:
                        aint(i)
                    if s == 4:
                        aq(i)
                if s + YB < 8:
                    if prev >= 0:
                        st2(prev, s + YB)
                elif i < NC:
                    st2(i, s + YB - 8)
                if nxt < NC:
                    if s == 5:
                        xq(nxt, 1)
                    if s >= 5:
                        st1(nxt, [s - 5])
                    if s == 7 and i > 0:
                        relu(nxt, 0)
                if s >= 6:
                    for w in wides_v[s - 6 :: 2]:
                        widen(*w)
